import numpy as np
import ml_dtypes


def mxq(x, axis, fmt="e4m3"):
    dtype, down = {"e4m3": (ml_dtypes.float8_e4m3fn, 7), "e5m2": (ml_dtypes.float8_e5m2, 14)}[fmt]
    v = np.moveaxis(np.asarray(x, np.float32).astype(ml_dtypes.bfloat16).astype(np.float64), axis, -1)
    blocks = v.reshape(v.shape[:-1] + (-1, 32))
    amax = np.abs(blocks).max(-1, keepdims=True)
    byte = np.maximum(np.where(amax > 0, np.frexp(amax)[1] - 1 + 127, 0) - down, 1)
    scale = np.exp2(byte - 127.0)
    codes = (blocks / scale).astype(np.float32).astype(dtype).astype(np.float64)
    return np.moveaxis((codes * scale).reshape(v.shape), -1, axis)


WIDE = False


def mx_kscale(k):
    if not WIDE:
        return np.ones(k)
    levels = np.array([30, -30])
    if k % 512:
        return np.exp2(np.random.permutation(np.resize(levels, k // 32))).repeat(32)
    a = np.empty((k // 512, 16))
    for p in range(k // 512):
        a[p, :8] = np.random.permutation(np.resize(levels, 8))
        for g in range(8):
            far = levels[np.abs(levels - a[p, g]) >= 10]
            a[p, g + 8] = far[np.random.randint(len(far))]
    return np.exp2(a.ravel()).repeat(32)


def f64(x):
    return np.asarray(x).astype(np.float64)


def striped(idx):
    return np.tile(np.asarray(idx).reshape(-1, 16).T, (8, 1)).astype(np.uint16)


def unstriped(offs):
    return offs[:16].T.reshape(-1).astype(np.int64)


E2M1 = np.array([0.0, 0.5, 1.0, 1.5, 2.0, 3.0, 4.0, 6.0, -0.0, -0.5, -1.0, -1.5, -2.0, -3.0, -4.0, -6.0])


def pack_weight(w, fmt):
    k, n = w.shape
    w = f64(np.asarray(w, np.float32).astype(ml_dtypes.bfloat16)).reshape(k // 32, 32, n)
    amax = np.abs(w).max(1)
    if fmt == "e4m3":
        byte = np.frexp(amax)[1] - 1 + 127 - 7
    else:
        mant, ex = np.frexp(amax / 6.0)
        byte = np.where(mant > 0.5, ex, ex - 1) + 127
    byte = np.clip(np.where(amax > 0, byte, 1), 1, 254)
    scaled = (w * np.exp2(127.0 - byte)[:, None, :]).reshape(k, n).astype(np.float32)
    by_word = np.ascontiguousarray(scaled.reshape(k // 512, 128, 4, n).transpose(0, 1, 3, 2))
    if fmt == "e4m3":
        words = by_word.astype(ml_dtypes.float8_e4m3fn).view(np.uint8)
    else:
        c = by_word.astype(ml_dtypes.float4_e2m1fn).view(np.uint8) & 0xF
        words = (c[..., 0::2] | (c[..., 1::2] << 4)).reshape(k // 512, 128, 2 * n)
    return np.ascontiguousarray(words), np.ascontiguousarray(byte.astype(np.uint8).reshape(k // 512, 16, n))


def unpack_weight(words, scales, fmt):
    g, _, n = scales.shape
    words = np.ascontiguousarray(words).reshape(g, 128, n, -1)
    if fmt == "e4m3":
        vals = words.view(ml_dtypes.float8_e4m3fn).astype(np.float64)
    else:
        nib = np.empty((g, 128, n, 4), np.uint8)
        nib[..., 0::2] = words & 0xF
        nib[..., 1::2] = words >> 4
        vals = E2M1[nib]
    vals = vals * np.repeat(np.exp2(scales.astype(np.float64) - 127.0), 8, axis=1)[..., None]
    return vals.transpose(0, 1, 3, 2).reshape(g * 512, n)


K, N, T, J, R = 512, 512, 2048, 512, 128


def setup_inputs():
    n = np.random.standard_normal
    idx = np.random.permutation(T)[:J]
    fj = mx_kscale(J)
    fk = mx_kscale(K)
    tj = np.ones(T)
    tj[idx] = fj
    drp = pack_weight(n((K, R)) * 1 / np.sqrt(K) / fk[:, None], "e2m1")
    return {
        "xt": (n((K, T)) * tj * fk[:, None]).astype(np.float32),
        "g": (n((N, T)) * np.exp(0.5 * n((1, T))) / tj).astype(np.float32),
        "dr_words": drp[0],
        "dr_scales": drp[1],
        "old": (1.0 * n((R, N))).astype(np.float32),
        "offs": striped(idx),
    }


def reference(xt, g, dr_words, dr_scales, old, offs):
    idx = unstriped(offs)
    dru = unpack_weight(dr_words, dr_scales, "e2m1")
    xj = f64(xt)[:, idx].T
    gj = f64(g)[:, idx].T
    xjq = mxq(xj, 0, "e4m3")
    gjq = mxq(gj, 0, "e5m2")
    w = xjq.T @ gjq
    wq = mxq(w, 0, "e4m3")
    v = dru.T @ wq
    y = 0.04 * v + 0.5 * f64(old)
    return y

@@ -1,0 +1,160 @@
+from contextlib import ExitStack
+
+import concourse.mybir as mybir
+from concourse.masks import make_identity
+
+K, N, T, J, R = 512, 512, 2048, 512, 128
+FLOPS = 2 * J * K * N + 2 * K * R * N
+
+F32 = mybir.dt.float32
+BF16 = mybir.dt.bfloat16
+I32 = mybir.dt.int32
+U32 = mybir.dt.uint32
+U16 = mybir.dt.uint16
+U8 = mybir.dt.uint8
+E4M3 = mybir.dt.float8_e4m3fn_x4
+E5M2 = mybir.dt.float8_e5m2_x4
+E2M1 = mybir.dt.float4_e2m1fn_x4
+MULT = mybir.AluOpType.mult
+ADD = mybir.AluOpType.add
+
+P = 128
+BLOCKS = 4
+
+
+ROW_BYTES = 4 * T
+
+
+def tile_moe_expert_wgrad_directions_kernel(tc, xt, g, dr_words, dr_scales, old, offs, out):
+    nc = tc.nc
+    with ExitStack() as ctx:
+        keep = ctx.enter_context(tc.tile_pool(name="keep", bufs=1))
+        rows = ctx.enter_context(tc.tile_pool(name="rows", bufs=1))
+        psum = ctx.enter_context(tc.psum_pool(name="psum", bufs=2))
+
+        offsets = keep.tile([P, J // 16], U16, name="offsets")
+        x_rows = [keep.tile([P, T], F32, name="x_rows%d" % b) for b in range(BLOCKS)]
+        g_rows = [
+            rows.tile([P, T], F32, name="g_rows%d" % b, offset=b * ROW_BYTES, align_bytes=64) for b in range(BLOCKS)
+        ]
+        dr_codes = keep.tile([P, 2 * R], U8, name="dr_codes", align_bytes=64)
+        dr_plane = keep.tile([P, R], U8, name="dr_plane", align_bytes=64)
+        old_sb = keep.tile([P, N], F32, name="old_sb")
+        half_old = keep.tile([P, N], F32, name="half_old")
+        ident = keep.tile([P, P], F32, name="ident")
+
+        def behind(b, place, shape, dtype, name):
+            if b is None:
+                return keep.tile(shape, dtype, name=name, align_bytes=64)
+            return rows.tile(shape, dtype, name=name, offset=b * ROW_BYTES + place, align_bytes=64)
+
+        nc.vector.memset(dr_plane[:].bitcast(I32), 0)
+        nc.sync.dma_start(x_rows[0][:], xt[0:P, :])
+        nc.sync.dma_start(offsets[:], offs)
+        nc.sync.dma_start(x_rows[1][:], xt[P : 2 * P, :])
+        nc.sync.dma_start(dr_codes[:].bitcast(I32), dr_words[0].bitcast(I32))
+        for i in range(4):
+            nc.sync.dma_start(dr_plane[i:P:32, :].bitcast(I32), dr_scales[0, i:16:4, :].bitcast(I32))
+        for b in range(2, BLOCKS):
+            nc.sync.dma_start(x_rows[b][:], xt[b * P : (b + 1) * P, :])
+        for b in range(BLOCKS):
+            nc.sync.dma_start(g_rows[b][:], g[b * P : (b + 1) * P, :])
+        nc.sync.dma_start(old_sb[:], old)
+        make_identity(nc, ident[:])
+
+        def gather(window, name):
+            picked = keep.tile([P, J], BF16, name=name, align_bytes=64)
+            nc.vector.tensor_copy(
+                picked[:].rearrange("f (u q r) -> f q u r", u=2, r=16), window[:].indirect(offsets[:])
+            )
+            return picked
+
+        def turn(halves, tag, grouped, copy):
+            words = halves[:].bitcast(F32)
+            turned = psum.tile([P, 2, P], F32, name=tag)
+            for u in range(2):
+                nc.tensor.transpose(turned[:, u, :], words[:, u * P : (u + 1) * P], ident[:])
+            copy(grouped.bitcast(F32).rearrange("p (c u) -> p c u", u=2), turned[:].rearrange("p u c -> p c u"))
+
+        x_grouped = keep.tile([P, 4 * K], BF16, name="x_grouped", align_bytes=64)
+        for b in range(BLOCKS):
+            picked = gather(x_rows[b], "x_picked%d" % b)
+            turn(picked, "turned_in", x_grouped[:, 4 * P * b : 4 * P * (b + 1)], nc.scalar.copy)
+
+        g_grouped = []
+
+        def front(b):
+            grouped = keep.tile([P, 4 * P], BF16, name="g_grouped%d" % b, align_bytes=64)
+            turn(gather(g_rows[b], "g_picked%d" % b), "turned_in", grouped[:], nc.scalar.copy)
+            g_grouped.append(grouped)
+
+        front(0)
+        x_codes = behind(0, 0, [P, K], U32, "x_codes")
+        x_plane = keep.tile([P, K], U8, name="x_plane", align_bytes=64)
+        nc.vector.quantize_mx(out=x_codes[:].bitcast(E4M3), scales=x_plane[:], in_=x_grouped[:])
+
+        w_grouped = []
+
+        def middle(b):
+            last = b == BLOCKS - 1
+            g_codes = behind(None if last else b + 1, 0, [P, P], U32, "g_codes%d" % b)
+            g_plane = keep.tile([P, P], U8, name="g_plane%d" % b, align_bytes=64)
+            nc.vector.quantize_mx(out=g_codes[:].bitcast(E5M2), scales=g_plane[:], in_=g_grouped[b][:])
+            w_t = psum.tile([P, K], F32, name="w_t")
+            nc.tensor.matmul_mx(
+                out=w_t[:],
+                lhsT=g_codes[:].bitcast(E5M2),
+                lhsT_scale=g_plane[:],
+                rhs=x_codes[:].bitcast(E4M3),
+                rhs_scale=x_plane[:],
+                start=True,
+                stop=True,
+            )
+            w_halves = keep.tile([P, K], BF16, name="w_halves%d" % b, align_bytes=64)
+            by_half = w_t[:].rearrange("n (p u e) -> n u p e", u=2, e=2)
+            for u in range(2):
+                nc.scalar.copy(
+                    w_halves[:, u * 256 : (u + 1) * 256].rearrange("n (p e) -> n p e", e=2), by_half[:, u, :, :]
+                )
+            return w_halves
+
+        def regroup(b, w_halves):
+            grouped = behind(3 if b == 1 else None, 2048, [P, 4 * P], BF16, "w_grouped%d" % b)
+            turn(w_halves, "turned_w", grouped[:], nc.vector.tensor_copy if b in (1, 2) else nc.scalar.copy)
+            w_grouped.append(grouped)
+
+        def back(b):
+            cols = slice(b * P, (b + 1) * P)
+            w_codes = behind(3 if b == 0 else None, 1024, [P, P], U32, "w_codes%d" % b)
+            w_plane = keep.tile([P, P], U8, name="w_plane%d" % b, align_bytes=64)
+            nc.vector.quantize_mx(out=w_codes[:].bitcast(E4M3), scales=w_plane[:], in_=w_grouped[b][:])
+            v = psum.tile([P, P], F32, name="v")
+            nc.tensor.matmul_mx(
+                out=v[:],
+                lhsT=dr_codes[:].bitcast(E2M1),
+                lhsT_scale=dr_plane[:],
+                rhs=w_codes[:].bitcast(E4M3),
+                rhs_scale=w_plane[:],
+                start=True,
+                stop=True,
+            )
+            result = keep.tile([P, P], F32, name="result%d" % b)
+            nc.vector.scalar_tensor_tensor(result[:], v[:], 0.04, half_old[:, cols], MULT, ADD)
+            nc.sync.dma_start(out[:, cols], result[:])
+
+        front(1)
+        h0 = middle(0)
+        front(2)
+        h1 = middle(1)
+        regroup(0, h0)
+        front(3)
+        h2 = middle(2)
+        h3 = middle(3)
+        nc.vector.tensor_scalar(half_old[:], old_sb[:], 0.5, None, MULT)
+        regroup(1, h1)
+        back(0)
+        back(1)
+        regroup(2, h2)
+        regroup(3, h3)
+        back(2)
+        back(3)

@@ -23,84 +23,83 @@ BLOCKS = 4
 
 
 ROW_BYTES = 4 * T
+BANK = 2048
 
 
 def tile_moe_expert_wgrad_directions_kernel(tc, xt, g, dr_words, dr_scales, old, offs, out):
     nc = tc.nc
     with ExitStack() as ctx:
         keep = ctx.enter_context(tc.tile_pool(name="keep", bufs=1))
-        rows = ctx.enter_context(tc.tile_pool(name="rows", bufs=1))
-        psum = ctx.enter_context(tc.psum_pool(name="psum", bufs=2))
+        placed = ctx.enter_context(tc.tile_pool(name="placed", bufs=1))
+        psum = ctx.enter_context(tc.psum_pool(name="psum", bufs=1))
+
+        def at(offset, shape, dtype, name):
+            if offset is None:
+                return keep.tile(shape, dtype, name=name, align_bytes=64)
+            return placed.tile(shape, dtype, name=name, offset=offset, align_bytes=64)
+
+        def bank(index, shape, name):
+            return psum.tile(shape, F32, name=name, offset=index * BANK)
+
+        def g_rows_at(b):
+            return b * ROW_BYTES
+
+        def g_grouped_at(b):
+            return BLOCKS * ROW_BYTES + b * 2048
 
         offsets = keep.tile([P, J // 16], U16, name="offsets")
         x_rows = [keep.tile([P, T], F32, name="x_rows%d" % b) for b in range(BLOCKS)]
-        g_rows = [
-            rows.tile([P, T], F32, name="g_rows%d" % b, offset=b * ROW_BYTES, align_bytes=64) for b in range(BLOCKS)
-        ]
+        g_rows = [at(g_rows_at(b), [P, T], F32, "g_rows%d" % b) for b in range(BLOCKS)]
         dr_codes = keep.tile([P, 2 * R], U8, name="dr_codes", align_bytes=64)
         dr_plane = keep.tile([P, R], U8, name="dr_plane", align_bytes=64)
         old_sb = keep.tile([P, N], F32, name="old_sb")
         half_old = keep.tile([P, N], F32, name="half_old")
         ident = keep.tile([P, P], F32, name="ident")
 
-        def behind(b, place, shape, dtype, name):
-            if b is None:
-                return keep.tile(shape, dtype, name=name, align_bytes=64)
-            return rows.tile(shape, dtype, name=name, offset=b * ROW_BYTES + place, align_bytes=64)
-
         nc.vector.memset(dr_plane[:].bitcast(I32), 0)
         nc.sync.dma_start(x_rows[0][:], xt[0:P, :])
         nc.sync.dma_start(offsets[:], offs)
-        nc.sync.dma_start(x_rows[1][:], xt[P : 2 * P, :])
+        for b in range(1, BLOCKS):
+            nc.sync.dma_start(x_rows[b][:], xt[b * P : (b + 1) * P, :])
+        nc.sync.dma_start(g_rows[0][:], g[0:P, :])
         nc.sync.dma_start(dr_codes[:].bitcast(I32), dr_words[0].bitcast(I32))
         for i in range(4):
             nc.sync.dma_start(dr_plane[i:P:32, :].bitcast(I32), dr_scales[0, i:16:4, :].bitcast(I32))
-        for b in range(2, BLOCKS):
-            nc.sync.dma_start(x_rows[b][:], xt[b * P : (b + 1) * P, :])
-        for b in range(BLOCKS):
+        for b in range(1, BLOCKS):
             nc.sync.dma_start(g_rows[b][:], g[b * P : (b + 1) * P, :])
         nc.sync.dma_start(old_sb[:], old)
         make_identity(nc, ident[:])
 
-        def gather(window, name):
-            picked = keep.tile([P, J], BF16, name=name, align_bytes=64)
+        def gather(window, name, offset):
+            picked = at(offset, [P, J], BF16, name)
             nc.vector.tensor_copy(
                 picked[:].rearrange("f (u q r) -> f q u r", u=2, r=16), window[:].indirect(offsets[:])
             )
             return picked
 
-        def turn(halves, tag, grouped, copy):
+        def turn(halves, index, name, grouped, copy):
             words = halves[:].bitcast(F32)
-            turned = psum.tile([P, 2, P], F32, name=tag)
+            turned = bank(index, [P, 2, P], name)
             for u in range(2):
                 nc.tensor.transpose(turned[:, u, :], words[:, u * P : (u + 1) * P], ident[:])
             copy(grouped.bitcast(F32).rearrange("p (c u) -> p c u", u=2), turned[:].rearrange("p u c -> p c u"))
 
         x_grouped = keep.tile([P, 4 * K], BF16, name="x_grouped", align_bytes=64)
         for b in range(BLOCKS):
-            picked = gather(x_rows[b], "x_picked%d" % b)
-            turn(picked, "turned_in", x_grouped[:, 4 * P * b : 4 * P * (b + 1)], nc.scalar.copy)
+            picked = gather(x_rows[b], "x_picked%d" % b, None)
+            turn(picked, b % 2, "x_turned%d" % b, x_grouped[:, 4 * P * b : 4 * P * (b + 1)], nc.scalar.copy)
 
-        g_grouped = []
+        def front(b, picked_at):
+            grouped = at(g_grouped_at(b), [P, 4 * P], BF16, "g_grouped%d" % b)
+            picked = gather(g_rows[b], "g_picked%d" % b, picked_at)
+            turn(picked, b % 2, "g_turned%d" % b, grouped[:], nc.scalar.copy)
+            return grouped
 
-        def front(b):
-            grouped = keep.tile([P, 4 * P], BF16, name="g_grouped%d" % b, align_bytes=64)
-            turn(gather(g_rows[b], "g_picked%d" % b), "turned_in", grouped[:], nc.scalar.copy)
-            g_grouped.append(grouped)
-
-        front(0)
-        x_codes = behind(0, 0, [P, K], U32, "x_codes")
-        x_plane = keep.tile([P, K], U8, name="x_plane", align_bytes=64)
-        nc.vector.quantize_mx(out=x_codes[:].bitcast(E4M3), scales=x_plane[:], in_=x_grouped[:])
-
-        w_grouped = []
-
-        def middle(b):
-            last = b == BLOCKS - 1
-            g_codes = behind(None if last else b + 1, 0, [P, P], U32, "g_codes%d" % b)
+        def middle(b, grouped, codes_at, halves_at, copy):
+            g_codes = at(codes_at, [P, P], U32, "g_codes%d" % b)
             g_plane = keep.tile([P, P], U8, name="g_plane%d" % b, align_bytes=64)
-            nc.vector.quantize_mx(out=g_codes[:].bitcast(E5M2), scales=g_plane[:], in_=g_grouped[b][:])
-            w_t = psum.tile([P, K], F32, name="w_t")
+            nc.vector.quantize_mx(out=g_codes[:].bitcast(E5M2), scales=g_plane[:], in_=grouped[:])
+            w_t = bank(2 + b % 2, [P, K], "w_t%d" % b)
             nc.tensor.matmul_mx(
                 out=w_t[:],
                 lhsT=g_codes[:].bitcast(E5M2),
@@ -110,25 +109,18 @@ def tile_moe_expert_wgrad_directions_kernel(tc, xt, g, dr_words, dr_scales, old,
                 start=True,
                 stop=True,
             )
-            w_halves = keep.tile([P, K], BF16, name="w_halves%d" % b, align_bytes=64)
+            w_halves = at(halves_at, [P, K], BF16, "w_halves%d" % b)
             by_half = w_t[:].rearrange("n (p u e) -> n u p e", u=2, e=2)
             for u in range(2):
-                nc.scalar.copy(
-                    w_halves[:, u * 256 : (u + 1) * 256].rearrange("n (p e) -> n p e", e=2), by_half[:, u, :, :]
-                )
+                copy(w_halves[:, u * 256 : (u + 1) * 256].rearrange("n (p e) -> n p e", e=2), by_half[:, u, :, :])
             return w_halves
 
-        def regroup(b, w_halves):
-            grouped = behind(3 if b == 1 else None, 2048, [P, 4 * P], BF16, "w_grouped%d" % b)
-            turn(w_halves, "turned_w", grouped[:], nc.vector.tensor_copy if b in (1, 2) else nc.scalar.copy)
-            w_grouped.append(grouped)
-
-        def back(b):
-            cols = slice(b * P, (b + 1) * P)
-            w_codes = behind(3 if b == 0 else None, 1024, [P, P], U32, "w_codes%d" % b)
-            w_plane = keep.tile([P, P], U8, name="w_plane%d" % b, align_bytes=64)
-            nc.vector.quantize_mx(out=w_codes[:].bitcast(E4M3), scales=w_plane[:], in_=w_grouped[b][:])
-            v = psum.tile([P, P], F32, name="v")
+        def back(first, count, grouped, codes_at, index):
+            width = count * P
+            w_codes = at(codes_at, [P, width], U32, "w_codes%d" % first)
+            w_plane = keep.tile([P, width], U8, name="w_plane%d" % first, align_bytes=64)
+            nc.vector.quantize_mx(out=w_codes[:].bitcast(E4M3), scales=w_plane[:], in_=grouped[:])
+            v = bank(index, [P, width], "v%d" % first)
             nc.tensor.matmul_mx(
                 out=v[:],
                 lhsT=dr_codes[:].bitcast(E2M1),
@@ -138,23 +130,37 @@ def tile_moe_expert_wgrad_directions_kernel(tc, xt, g, dr_words, dr_scales, old,
                 start=True,
                 stop=True,
             )
-            result = keep.tile([P, P], F32, name="result%d" % b)
+            return v
+
+        def finish(first, count, v, result_at):
+            cols = slice(first * P, (first + count) * P)
+            result = at(result_at, [P, count * P], F32, "result%d" % first)
             nc.vector.scalar_tensor_tensor(result[:], v[:], 0.04, half_old[:, cols], MULT, ADD)
             nc.sync.dma_start(out[:, cols], result[:])
 
-        front(1)
-        h0 = middle(0)
-        front(2)
-        h1 = middle(1)
-        regroup(0, h0)
-        front(3)
-        h2 = middle(2)
-        h3 = middle(3)
+        w01 = at(None, [P, 8 * P], BF16, "w_grouped01")
+        w2 = at(None, [P, 4 * P], BF16, "w_grouped2")
+        w3 = at(None, [P, 4 * P], BF16, "w_grouped3")
+
+        g0 = front(0, None)
+        x_codes = at(g_rows_at(0), [P, K], U32, "x_codes")
+        x_plane = keep.tile([P, K], U8, name="x_plane", align_bytes=64)
+        nc.vector.quantize_mx(out=x_codes[:].bitcast(E4M3), scales=x_plane[:], in_=x_grouped[:])
+        g1 = front(1, None)
+        h0 = middle(0, g0, g_rows_at(1), None, nc.scalar.copy)
+        h1 = middle(1, g1, None, None, nc.scalar.copy)
+        g2 = front(2, g_grouped_at(1))
+        turn(h0, 4, "w_turned0", w01[:, : 4 * P], nc.scalar.copy)
+        turn(h1, 5, "w_turned1", w01[:, 4 * P :], nc.scalar.copy)
+        g3 = front(3, None)
+        h3 = middle(3, g3, None, None, nc.scalar.copy)
+        h2 = middle(2, g2, g_rows_at(3), g_grouped_at(3) - 512, nc.vector.tensor_copy)
+        v01 = back(0, 2, w01, g_rows_at(3) + 1024, 6)
         nc.vector.tensor_scalar(half_old[:], old_sb[:], 0.5, None, MULT)
-        regroup(1, h1)
-        back(0)
-        back(1)
-        regroup(2, h2)
-        regroup(3, h3)
-        back(2)
-        back(3)
+        finish(0, 2, v01, g_grouped_at(3) + 512)
+        turn(h2, 4, "w_turned2", w2[:], nc.vector.tensor_copy)
+        turn(h3, 5, "w_turned3", w3[:], nc.scalar.copy)
+        v2 = back(2, 1, w2, None, 0)
+        v3 = back(3, 1, w3, None, 7)
+        finish(2, 1, v2, None)
+        finish(3, 1, v3, None)

@@ -62,12 +62,12 @@ def tile_moe_expert_wgrad_directions_kernel(tc, xt, g, dr_words, dr_scales, old,
         for b in range(1, BLOCKS):
             nc.sync.dma_start(x_rows[b][:], xt[b * P : (b + 1) * P, :])
         nc.sync.dma_start(g_rows[0][:], g[0:P, :])
-        nc.sync.dma_start(dr_codes[:].bitcast(I32), dr_words[0].bitcast(I32))
-        for i in range(4):
-            nc.sync.dma_start(dr_plane[i:P:32, :].bitcast(I32), dr_scales[0, i:16:4, :].bitcast(I32))
         for b in range(1, BLOCKS):
             nc.sync.dma_start(g_rows[b][:], g[b * P : (b + 1) * P, :])
         nc.sync.dma_start(old_sb[:], old)
+        nc.sync.dma_start(dr_codes[:].bitcast(I32), dr_words[0].bitcast(I32))
+        for i in range(4):
+            nc.sync.dma_start(dr_plane[i:P:32, :].bitcast(I32), dr_scales[0, i:16:4, :].bitcast(I32))
         make_identity(nc, ident[:])
 
         def gather(window, name, offset):
@@ -149,15 +149,15 @@ def tile_moe_expert_wgrad_directions_kernel(tc, xt, g, dr_words, dr_scales, old,
         g1 = front(1, None)
         h0 = middle(0, g0, g_rows_at(1), None, nc.scalar.copy)
         h1 = middle(1, g1, None, None, nc.scalar.copy)
-        g2 = front(2, g_grouped_at(1))
         turn(h0, 4, "w_turned0", w01[:, : 4 * P], nc.scalar.copy)
+        g2 = front(2, g_grouped_at(1))
         turn(h1, 5, "w_turned1", w01[:, 4 * P :], nc.scalar.copy)
         g3 = front(3, None)
         h3 = middle(3, g3, None, None, nc.scalar.copy)
         h2 = middle(2, g2, g_rows_at(3), g_grouped_at(3) - 512, nc.vector.tensor_copy)
-        v01 = back(0, 2, w01, g_rows_at(3) + 1024, 6)
+        v01 = back(0, 2, w01, g_grouped_at(3) + 512, 6)
         nc.vector.tensor_scalar(half_old[:], old_sb[:], 0.5, None, MULT)
-        finish(0, 2, v01, g_grouped_at(3) + 512)
+        finish(0, 2, v01, None)
         turn(h2, 4, "w_turned2", w2[:], nc.vector.tensor_copy)
         turn(h3, 5, "w_turned3", w3[:], nc.scalar.copy)
         v2 = back(2, 1, w2, None, 0)

from contextlib import ExitStack

import concourse.mybir as mybir
from concourse.masks import make_identity

K, N, T, J, R = 512, 512, 2048, 512, 128
FLOPS = 2 * J * K * N + 2 * K * R * N

F32 = mybir.dt.float32
BF16 = mybir.dt.bfloat16
I32 = mybir.dt.int32
U32 = mybir.dt.uint32
U16 = mybir.dt.uint16
U8 = mybir.dt.uint8
E4M3 = mybir.dt.float8_e4m3fn_x4
E5M2 = mybir.dt.float8_e5m2_x4
E2M1 = mybir.dt.float4_e2m1fn_x4
MULT = mybir.AluOpType.mult
ADD = mybir.AluOpType.add

P = 128
BLOCKS = 4


ROW_BYTES = 4 * T
BANK = 2048


def tile_moe_expert_wgrad_directions_kernel(tc, xt, g, dr_words, dr_scales, old, offs, out):
    nc = tc.nc
    with ExitStack() as ctx:
        keep = ctx.enter_context(tc.tile_pool(name="keep", bufs=1))
        placed = ctx.enter_context(tc.tile_pool(name="placed", bufs=1))
        psum = ctx.enter_context(tc.psum_pool(name="psum", bufs=1))

        def at(offset, shape, dtype, name):
            if offset is None:
                return keep.tile(shape, dtype, name=name, align_bytes=64)
            return placed.tile(shape, dtype, name=name, offset=offset, align_bytes=64)

        def bank(index, shape, name):
            return psum.tile(shape, F32, name=name, offset=index * BANK)

        def g_rows_at(b):
            return b * ROW_BYTES

        def g_grouped_at(b):
            return BLOCKS * ROW_BYTES + b * 2048

        offsets = keep.tile([P, J // 16], U16, name="offsets")
        x_rows = [keep.tile([P, T], F32, name="x_rows%d" % b) for b in range(BLOCKS)]
        g_rows = [at(g_rows_at(b), [P, T], F32, "g_rows%d" % b) for b in range(BLOCKS)]
        dr_codes = keep.tile([P, 2 * R], U8, name="dr_codes", align_bytes=64)
        dr_plane = keep.tile([P, R], U8, name="dr_plane", align_bytes=64)
        old_sb = keep.tile([P, N], F32, name="old_sb")
        half_old = keep.tile([P, N], F32, name="half_old")
        ident = keep.tile([P, P], F32, name="ident")

        nc.vector.memset(dr_plane[:].bitcast(I32), 0)
        nc.sync.dma_start(x_rows[0][:], xt[0:P, :])
        nc.sync.dma_start(offsets[:], offs)
        for b in range(1, BLOCKS):
            nc.sync.dma_start(x_rows[b][:], xt[b * P : (b + 1) * P, :])
        nc.sync.dma_start(g_rows[0][:], g[0:P, :])
        for b in range(1, BLOCKS):
            nc.sync.dma_start(g_rows[b][:], g[b * P : (b + 1) * P, :])
        nc.sync.dma_start(old_sb[:], old)
        nc.sync.dma_start(dr_codes[:].bitcast(I32), dr_words[0].bitcast(I32))
        for i in range(4):
            nc.sync.dma_start(dr_plane[i:P:32, :].bitcast(I32), dr_scales[0, i:16:4, :].bitcast(I32))
        make_identity(nc, ident[:])

        def gather(window, name, offset):
            picked = at(offset, [P, J], BF16, name)
            nc.vector.tensor_copy(
                picked[:].rearrange("f (u q r) -> f q u r", u=2, r=16), window[:].indirect(offsets[:])
            )
            return picked

        def turn(halves, index, name, grouped, copy):
            words = halves[:].bitcast(F32)
            turned = bank(index, [P, 2, P], name)
            for u in range(2):
                nc.tensor.transpose(turned[:, u, :], words[:, u * P : (u + 1) * P], ident[:])
            copy(grouped.bitcast(F32).rearrange("p (c u) -> p c u", u=2), turned[:].rearrange("p u c -> p c u"))

        x_grouped = keep.tile([P, 4 * K], BF16, name="x_grouped", align_bytes=64)
        for b in range(BLOCKS):
            picked = gather(x_rows[b], "x_picked%d" % b, None)
            turn(picked, b % 2, "x_turned%d" % b, x_grouped[:, 4 * P * b : 4 * P * (b + 1)], nc.scalar.copy)

        def front(b, picked_at):
            grouped = at(g_grouped_at(b), [P, 4 * P], BF16, "g_grouped%d" % b)
            picked = gather(g_rows[b], "g_picked%d" % b, picked_at)
            turn(picked, b % 2, "g_turned%d" % b, grouped[:], nc.scalar.copy)
            return grouped

        def middle(b, grouped, codes_at, halves_at, copy):
            g_codes = at(codes_at, [P, P], U32, "g_codes%d" % b)
            g_plane = keep.tile([P, P], U8, name="g_plane%d" % b, align_bytes=64)
            nc.vector.quantize_mx(out=g_codes[:].bitcast(E5M2), scales=g_plane[:], in_=grouped[:])
            w_t = bank(2 + b % 2, [P, K], "w_t%d" % b)
            nc.tensor.matmul_mx(
                out=w_t[:],
                lhsT=g_codes[:].bitcast(E5M2),
                lhsT_scale=g_plane[:],
                rhs=x_codes[:].bitcast(E4M3),
                rhs_scale=x_plane[:],
                start=True,
                stop=True,
            )
            w_halves = at(halves_at, [P, K], BF16, "w_halves%d" % b)
            by_half = w_t[:].rearrange("n (p u e) -> n u p e", u=2, e=2)
            for u in range(2):
                copy(w_halves[:, u * 256 : (u + 1) * 256].rearrange("n (p e) -> n p e", e=2), by_half[:, u, :, :])
            return w_halves

        def back(first, count, grouped, codes_at, index):
            width = count * P
            w_codes = at(codes_at, [P, width], U32, "w_codes%d" % first)
            w_plane = keep.tile([P, width], U8, name="w_plane%d" % first, align_bytes=64)
            nc.vector.quantize_mx(out=w_codes[:].bitcast(E4M3), scales=w_plane[:], in_=grouped[:])
            v = bank(index, [P, width], "v%d" % first)
            nc.tensor.matmul_mx(
                out=v[:],
                lhsT=dr_codes[:].bitcast(E2M1),
                lhsT_scale=dr_plane[:],
                rhs=w_codes[:].bitcast(E4M3),
                rhs_scale=w_plane[:],
                start=True,
                stop=True,
            )
            return v

        def finish(first, count, v, result_at):
            cols = slice(first * P, (first + count) * P)
            result = at(result_at, [P, count * P], F32, "result%d" % first)
            nc.vector.scalar_tensor_tensor(result[:], v[:], 0.04, half_old[:, cols], MULT, ADD)
            nc.sync.dma_start(out[:, cols], result[:])

        w01 = at(None, [P, 8 * P], BF16, "w_grouped01")
        w2 = at(None, [P, 4 * P], BF16, "w_grouped2")
        w3 = at(None, [P, 4 * P], BF16, "w_grouped3")

        g0 = front(0, None)
        x_codes = at(g_rows_at(0), [P, K], U32, "x_codes")
        x_plane = keep.tile([P, K], U8, name="x_plane", align_bytes=64)
        nc.vector.quantize_mx(out=x_codes[:].bitcast(E4M3), scales=x_plane[:], in_=x_grouped[:])
        g1 = front(1, None)
        h0 = middle(0, g0, g_rows_at(1), None, nc.scalar.copy)
        h1 = middle(1, g1, None, None, nc.scalar.copy)
        turn(h0, 4, "w_turned0", w01[:, : 4 * P], nc.scalar.copy)
        g2 = front(2, g_grouped_at(1))
        turn(h1, 5, "w_turned1", w01[:, 4 * P :], nc.scalar.copy)
        g3 = front(3, None)
        h3 = middle(3, g3, None, None, nc.scalar.copy)
        h2 = middle(2, g2, g_rows_at(3), g_grouped_at(3) - 512, nc.vector.tensor_copy)
        v01 = back(0, 2, w01, g_grouped_at(3) + 512, 6)
        nc.vector.tensor_scalar(half_old[:], old_sb[:], 0.5, None, MULT)
        finish(0, 2, v01, None)
        turn(h2, 4, "w_turned2", w2[:], nc.vector.tensor_copy)
        turn(h3, 5, "w_turned3", w3[:], nc.scalar.copy)
        v2 = back(2, 1, w2, None, 0)
        v3 = back(3, 1, w3, None, 7)
        finish(2, 1, v2, None)
        finish(3, 1, v3, None)
